import numpy as np
import ml_dtypes


def mxq(x, axis, fmt="e4m3"):
    dtype, down = {"e4m3": (ml_dtypes.float8_e4m3fn, 7), "e5m2": (ml_dtypes.float8_e5m2, 14)}[fmt]
    v = np.moveaxis(np.asarray(x, np.float32).astype(ml_dtypes.bfloat16).astype(np.float64), axis, -1)
    blocks = v.reshape(v.shape[:-1] + (-1, 32))
    amax = np.abs(blocks).max(-1, keepdims=True)
    byte = np.maximum(np.where(amax > 0, np.frexp(amax)[1] - 1 + 127, 0) - down, 1)
    scale = np.exp2(byte - 127.0)
    codes = (blocks / scale).astype(np.float32).astype(dtype).astype(np.float64)
    return np.moveaxis((codes * scale).reshape(v.shape), -1, axis)


WIDE = False


def mx_kscale(k):
    if not WIDE:
        return np.ones(k)
    levels = np.array([10, -10, 5, -5, 0])
    if k % 512:
        return np.exp2(np.random.permutation(np.resize(levels, k // 32))).repeat(32)
    a = np.empty((k // 512, 16))
    for p in range(k // 512):
        a[p, :8] = np.random.permutation(np.resize(levels, 8))
        for g in range(8):
            far = levels[np.abs(levels - a[p, g]) >= 10]
            a[p, g + 8] = far[np.random.randint(len(far))]
    return np.exp2(a.ravel()).repeat(32)


def f64(x):
    return np.asarray(x).astype(np.float64)


def striped(idx):
    return np.tile(np.asarray(idx).reshape(-1, 16).T, (8, 1)).astype(np.uint16)


def unstriped(offs):
    return offs[:16].T.reshape(-1).astype(np.int64)


E2M1 = np.array([0.0, 0.5, 1.0, 1.5, 2.0, 3.0, 4.0, 6.0, -0.0, -0.5, -1.0, -1.5, -2.0, -3.0, -4.0, -6.0])


def pack_weight(w, fmt):
    k, n = w.shape
    w = f64(np.asarray(w, np.float32).astype(ml_dtypes.bfloat16)).reshape(k // 32, 32, n)
    amax = np.abs(w).max(1)
    if fmt == "e4m3":
        byte = np.frexp(amax)[1] - 1 + 127 - 7
    else:
        mant, ex = np.frexp(amax / 6.0)
        byte = np.where(mant > 0.5, ex, ex - 1) + 127
    byte = np.clip(np.where(amax > 0, byte, 1), 1, 254)
    scaled = (w * np.exp2(127.0 - byte)[:, None, :]).reshape(k, n).astype(np.float32)
    by_word = np.ascontiguousarray(scaled.reshape(k // 512, 128, 4, n).transpose(0, 1, 3, 2))
    if fmt == "e4m3":
        words = by_word.astype(ml_dtypes.float8_e4m3fn).view(np.uint8)
    else:
        c = by_word.astype(ml_dtypes.float4_e2m1fn).view(np.uint8) & 0xF
        words = (c[..., 0::2] | (c[..., 1::2] << 4)).reshape(k // 512, 128, 2 * n)
    return np.ascontiguousarray(words), np.ascontiguousarray(byte.astype(np.uint8).reshape(k // 512, 16, n))


def unpack_weight(words, scales, fmt):
    g, _, n = scales.shape
    words = np.ascontiguousarray(words).reshape(g, 128, n, -1)
    if fmt == "e4m3":
        vals = words.view(ml_dtypes.float8_e4m3fn).astype(np.float64)
    else:
        nib = np.empty((g, 128, n, 4), np.uint8)
        nib[..., 0::2] = words & 0xF
        nib[..., 1::2] = words >> 4
        vals = E2M1[nib]
    vals = vals * np.repeat(np.exp2(scales.astype(np.float64) - 127.0), 8, axis=1)[..., None]
    return vals.transpose(0, 1, 3, 2).reshape(g * 512, n)


def bf(x):
    return np.asarray(x, np.float32).astype(ml_dtypes.bfloat16)


def planes(Y):
    r, m = Y.shape
    b = f64(bf(Y)).reshape(r // 32, 32, m)
    amax = np.abs(b).max(1)
    byte = np.clip(np.where(amax > 0, np.frexp(amax)[1] - 1 + 127 - 7, 1), 1, 254)
    codes = (b * np.exp2(127.0 - byte)[:, None, :]).reshape(r, m).astype(np.float32).astype(ml_dtypes.float8_e4m3fn).view(np.uint8)
    words = codes.reshape(r // 512, 128, 4, m).transpose(0, 1, 3, 2)
    return np.ascontiguousarray(words), np.ascontiguousarray(byte.astype(np.uint8).reshape(r // 512, 16, m))


D, T, I, J, G = 512, 2048, 512, 1024, 128


def setup_inputs():
    n = np.random.standard_normal
    idx = np.random.permutation(T)[:I]
    idx2 = np.random.permutation(T)[:J]
    fd = mx_kscale(D)
    entsp = pack_weight(n((D, T)) / fd[:, None], "e2m1")
    return {
        "ment": (n((D, G)) * 1.0 / np.sqrt(D) * fd[:, None]).astype(np.float32),
        "ents_words": entsp[0],
        "ents_scales": entsp[1],
        "comp": (n((D, T)) * 1.5 / np.sqrt(D) * fd[:, None]).astype(np.float32),
        "trust": (np.random.uniform(0.5, 1.5, (1, G))).astype(np.float32),
        "offs": striped(idx),
        "offs2": striped(idx2),
    }


def reference(ment, ents_words, ents_scales, comp, trust, offs, offs2):
    idx = unstriped(offs)
    idx2 = unstriped(offs2)
    entsu = unpack_weight(ents_words, ents_scales, "e2m1")
    entsidxg = entsu[:, idx]
    mentq = mxq(f64(ment), 0, "e4m3")
    a = entsidxg.T @ mentq
    compidx2q = mxq(f64(comp)[:, idx2], 0, "e4m3")
    b = entsidxg.T @ compidx2q
    y = a + np.tanh(b.reshape(I, G, J // G).mean(axis=2)) * f64(trust)
    words, scales = planes(y)
    return y, words, scales

@@ -1,0 +1,141 @@
+from contextlib import ExitStack
+
+import concourse.mybir as mybir
+
+D, T, I, J, G = 512, 2048, 512, 1024, 128
+FLOPS = 2 * D * I * (J + G)
+
+F32 = mybir.dt.float32
+BF16 = mybir.dt.bfloat16
+I32 = mybir.dt.int32
+U32 = mybir.dt.uint32
+U16 = mybir.dt.uint16
+U8 = mybir.dt.uint8
+FP8X4 = mybir.dt.float8_e4m3fn_x4
+FP4X4 = mybir.dt.float4_e2m1fn_x4
+ACT = mybir.ActivationFunctionType
+ALU = mybir.AluOpType
+
+P = 128
+R = J // G
+CH = 256
+NCH = J // CH
+
+
+def tile_attend_coherence_pl_kernel(tc, ment, ents_words, ents_scales, comp, trust, offs, offs2, out_0, out_1, out_2):
+    nc = tc.nc
+    with ExitStack() as ctx:
+        keep = ctx.enter_context(tc.tile_pool(name="keep", bufs=1))
+        psum = ctx.enter_context(tc.psum_pool(name="psum", bufs=1))
+
+        offs_sb = keep.tile([P, I // 16], U16, name="offs_sb")
+        offs2_sb = keep.tile([P, J // 16], U16, name="offs2_sb")
+        ew = keep.tile([P, T], U16, name="ew", align_bytes=64)
+        es = keep.tile([P, T], U8, name="es", align_bytes=64)
+        warm_in = keep.tile([P, 1], F32, name="warm_in")
+        warm_out = keep.tile([P, 1], F32, name="warm_out")
+
+        nc.vector.memset(es[:].bitcast(I32), 0)
+        for q in range(4):
+            nc.scalar.dma_start(out=es[32 * q : 32 * q + 4, :].bitcast(I32), in_=ents_scales[0, 4 * q : 4 * q + 4, :].bitcast(I32))
+        nc.vector.memset(warm_in[:], 0.0)
+        nc.scalar.activation(out=warm_out[:], in_=warm_in[:], func=ACT.Tanh)
+
+        comp_v = comp.rearrange("(p t) n -> p t n", t=4)
+        chunks = [(0, 0, 1024, 1024), (0, 1024, 1024, 352), (1, 0, 1024, 1024), (1, 1024, 512, 0), (1, 1536, 256, 0), (1, 1792, 256, 96)]
+        raw = [keep.tile([P, 2, w], F32, name=f"raw{k}") for k, (u, c0, w, s) in enumerate(chunks)]
+        ment_raw = keep.tile([P, 4, G], F32, name="ment_raw")
+        trust_sb = keep.tile([P, G], F32, name="trust_sb")
+
+        nc.sync.dma_start(offs_sb[:], offs)
+        nc.sync.dma_start(offs2_sb[:], offs2)
+        for h in range(2):
+            nc.sync.dma_start(out=ew[:].bitcast(I32)[:, 512 * h : 512 * (h + 1)], in_=ents_words[0].bitcast(I32)[:, 512 * h : 512 * (h + 1)])
+        for k, (u, c0, w, s) in enumerate(chunks):
+            nc.sync.dma_start(out=raw[k][:], in_=comp_v[:, 2 * u : 2 * u + 2, c0 : c0 + w])
+        nc.sync.dma_start(out=ment_raw[:], in_=ment.rearrange("(p t) g -> p t g", t=4))
+        nc.sync.dma_start(out=trust_sb[:], in_=trust[0].partition_broadcast(P))
+
+        ewg = keep.tile([P, I], U16, name="ewg", align_bytes=64)
+        esg = keep.tile([P, I], U8, name="esg", align_bytes=64)
+        ewd = keep.tile([P, I], U16, name="ewd", align_bytes=64)
+        esd = keep.tile([P, I], U8, name="esd", align_bytes=64)
+        nc.vector.tensor_copy(out=ewg[:], in_=ew[:].indirect(offs_sb[:]))
+        nc.vector.tensor_copy(out=esg[:], in_=es[:].indirect(offs_sb[:]))
+        nc.vector.tensor_copy(out=ewd[:].rearrange("p (t m) -> p t m", t=4), in_=ewg[:].rearrange("p (m t) -> p t m", t=4))
+        nc.vector.tensor_copy(out=esd[:].rearrange("p (t m) -> p m t", t=4), in_=esg[:].rearrange("p (m t) -> p m t", t=4))
+
+        win = [keep.tile([P, T], F32, name=f"win{u}", align_bytes=64) for u in range(2)]
+        gat = [keep.tile([P, 2, CH], F32, name=f"gat{c}", align_bytes=64) for c in range(NCH)]
+
+        def cast(k):
+            u, c0, w, s = chunks[k]
+            dst = win[u][:].bitcast(BF16).rearrange("p (n e) -> p n e", e=2)
+            src = raw[k][:].rearrange("p e n -> p n e")
+            if s > 0:
+                nc.scalar.activation(out=dst[:, c0 : c0 + s, :], in_=src[:, 0:s, :], func=ACT.Copy)
+            if s < w:
+                nc.vector.tensor_copy(out=dst[:, c0 + s : c0 + w, :], in_=src[:, s:w, :])
+
+        def gather(u, c):
+            nc.vector.tensor_copy(out=gat[c][:, u, :], in_=win[u][:].indirect(offs2_sb[:, c * (CH // 16) : (c + 1) * (CH // 16)]))
+
+        cast(0)
+        cast(1)
+        cast(2)
+        for c in range(NCH):
+            gather(0, c)
+        for k in range(3, len(chunks)):
+            cast(k)
+
+        ment16 = keep.tile([P, G, 4], BF16, name="ment16", align_bytes=64)
+        nc.scalar.activation(out=ment16[:], in_=ment_raw[:].rearrange("p t g -> p g t"), func=ACT.Copy)
+
+        x16 = keep.tile([P, R, G * 4], BF16, name="x16", align_bytes=64)
+        xw = x16[:].bitcast(F32).rearrange("p (h q) (g u) -> p h g u q", q=4, u=2)
+        gc = CH // R
+        for c in range(NCH):
+            gather(1, c)
+            nc.scalar.copy(out=xw[:, :, gc * c : gc * (c + 1), :, :], in_=gat[c][:].rearrange("p u (g h q) -> p h g u q", h=2, q=4))
+
+        mc = keep.tile([P, G], U32, name="mc", align_bytes=64)
+        ms = keep.tile([P, G], U8, name="ms", align_bytes=64)
+        nc.vector.quantize_mx(out=mc[:].bitcast(FP8X4), scales=ms[:], in_=ment16[:].rearrange("p g t -> p (g t)"))
+        a_ps = psum.tile([P, 4, G], F32, name="a_ps")
+        for t in range(4):
+            nc.tensor.matmul_mx(out=a_ps[:, t, :], lhsT=ewd[:, P * t : P * (t + 1)].bitcast(FP4X4), lhsT_scale=esd[:, P * t : P * (t + 1)],
+                                rhs=mc[:].bitcast(FP8X4), rhs_scale=ms[:], start=True, stop=True)
+
+        xc = keep.tile([P, R, G], U32, name="xc", align_bytes=64)
+        xs = keep.tile([P, R, G], U8, name="xs", align_bytes=64)
+        for r in range(R):
+            nc.vector.quantize_mx(out=xc[:, r, :].bitcast(FP8X4), scales=xs[:, r, :], in_=x16[:, r, :])
+
+        y = keep.tile([P, 4, G], F32, name="y")
+        y16 = keep.tile([P, G, 4], BF16, name="y16", align_bytes=64)
+        out_v = out_0.rearrange("(p t) g -> p t g", t=4)
+        for t in range(4):
+            b_ps = psum.tile([P, G], F32, name=f"b_ps{t}")
+            for r in range(R):
+                nc.tensor.matmul_mx(out=b_ps[:], lhsT=ewd[:, P * t : P * (t + 1)].bitcast(FP4X4), lhsT_scale=esd[:, P * t : P * (t + 1)],
+                                    rhs=xc[:, r, :].bitcast(FP8X4), rhs_scale=xs[:, r, :], start=(r == 0), stop=(r == R - 1))
+            th = keep.tile([P, G], F32, name=f"th{t}")
+            tm = keep.tile([P, G], F32, name=f"tm{t}")
+            nc.scalar.activation(out=th[:], in_=b_ps[:], func=ACT.Tanh, scale=1.0 / R)
+            nc.vector.tensor_tensor(out=tm[:], in0=th[:], in1=trust_sb[:], op=ALU.mult)
+            if t >= 2:
+                nc.vector.tensor_tensor(out=y16[:, :, t], in0=tm[:], in1=a_ps[:, t, :], op=ALU.add)
+            nc.vector.tensor_tensor(out=y[:, t, :], in0=tm[:], in1=a_ps[:, t, :], op=ALU.add)
+            if t == 1:
+                nc.scalar.activation(out=y16[:, :, 0:2], in_=y[:, 0:2, :].rearrange("p t g -> p g t"), func=ACT.Copy)
+            if t == 2:
+                nc.sync.dma_start(out=out_v[:, 0:3, :], in_=y[:, 0:3, :])
+        nc.sync.dma_start(out=out_v[:, 3, :], in_=y[:, 3, :])
+
+        yc = keep.tile([P, G], U32, name="yc", align_bytes=64)
+        ys = keep.tile([P, G], U8, name="ys", align_bytes=64)
+        nc.vector.quantize_mx(out=yc[:].bitcast(FP8X4), scales=ys[:], in_=y16[:].rearrange("p g t -> p (g t)"))
+        nc.sync.dma_start(out=out_1[0].rearrange("p c r -> p (c r)").bitcast(I32), in_=yc[:].bitcast(I32))
+        for q in range(4):
+            eng = nc.scalar if q < 2 else nc.sync
+            eng.dma_start(out=out_2[0, 4 * q : 4 * q + 4, :].bitcast(I32), in_=ys[32 * q : 32 * q + 4, :].bitcast(I32))

@@ -26,6 +26,7 @@ def tile_attend_coherence_pl_kernel(tc, ment, ents_words, ents_scales, comp, tru
     nc = tc.nc
     with ExitStack() as ctx:
         keep = ctx.enter_context(tc.tile_pool(name="keep", bufs=1))
+        shared = ctx.enter_context(tc.tile_pool(name="shared", bufs=1))
         psum = ctx.enter_context(tc.psum_pool(name="psum", bufs=1))
 
         offs_sb = keep.tile([P, I // 16], U16, name="offs_sb")
@@ -35,35 +36,37 @@ def tile_attend_coherence_pl_kernel(tc, ment, ents_words, ents_scales, comp, tru
         warm_in = keep.tile([P, 1], F32, name="warm_in")
         warm_out = keep.tile([P, 1], F32, name="warm_out")
 
-        nc.vector.memset(es[:].bitcast(I32), 0)
-        for q in range(4):
-            nc.scalar.dma_start(out=es[32 * q : 32 * q + 4, :].bitcast(I32), in_=ents_scales[0, 4 * q : 4 * q + 4, :].bitcast(I32))
         nc.vector.memset(warm_in[:], 0.0)
         nc.scalar.activation(out=warm_out[:], in_=warm_in[:], func=ACT.Tanh)
+        nc.vector.memset(es[:].bitcast(I32), 0)
+        nc.scalar.dma_start(out=es[0:P:8, :].bitcast(I32), in_=ents_scales[0].bitcast(I32))
 
         comp_v = comp.rearrange("(p t) n -> p t n", t=4)
-        chunks = [(0, 0, 1024, 1024), (0, 1024, 1024, 352), (1, 0, 1024, 1024), (1, 1024, 512, 0), (1, 1536, 256, 0), (1, 1792, 256, 96)]
+        chunks = [(0, 0, 512, 512), (0, 512, 512, 512), (0, 1024, 512, 256), (0, 1536, 512, 192), (1, 0, 512, 512), (1, 512, 512, 512), (1, 1024, 512, 192), (1, 1536, 256, 96), (1, 1792, 256, 96)]
         raw = [keep.tile([P, 2, w], F32, name=f"raw{k}") for k, (u, c0, w, s) in enumerate(chunks)]
-        ment_raw = keep.tile([P, 4, G], F32, name="ment_raw")
-        trust_sb = keep.tile([P, G], F32, name="trust_sb")
+        x16 = [shared.tile([P, 4, G * 4], BF16, name=f"x16_{h}", align_bytes=64, offset=4096 * h) for h in range(2)]
+        ment_raw = shared.tile([P, 4, G], F32, name="ment_raw", align_bytes=64, offset=3072)
 
-        nc.sync.dma_start(offs_sb[:], offs)
-        nc.sync.dma_start(offs2_sb[:], offs2)
         for h in range(2):
             nc.sync.dma_start(out=ew[:].bitcast(I32)[:, 512 * h : 512 * (h + 1)], in_=ents_words[0].bitcast(I32)[:, 512 * h : 512 * (h + 1)])
+        nc.sync.dma_start(offs_sb[:], offs)
+        nc.sync.dma_start(offs2_sb[:], offs2)
         for k, (u, c0, w, s) in enumerate(chunks):
             nc.sync.dma_start(out=raw[k][:], in_=comp_v[:, 2 * u : 2 * u + 2, c0 : c0 + w])
         nc.sync.dma_start(out=ment_raw[:], in_=ment.rearrange("(p t) g -> p t g", t=4))
-        nc.sync.dma_start(out=trust_sb[:], in_=trust[0].partition_broadcast(P))
 
         ewg = keep.tile([P, I], U16, name="ewg", align_bytes=64)
-        esg = keep.tile([P, I], U8, name="esg", align_bytes=64)
+        esg = keep.tile([P, I], U8, name="esg", tag="short", align_bytes=64)
         ewd = keep.tile([P, I], U16, name="ewd", align_bytes=64)
         esd = keep.tile([P, I], U8, name="esd", align_bytes=64)
         nc.vector.tensor_copy(out=ewg[:], in_=ew[:].indirect(offs_sb[:]))
         nc.vector.tensor_copy(out=esg[:], in_=es[:].indirect(offs_sb[:]))
-        nc.vector.tensor_copy(out=ewd[:].rearrange("p (t m) -> p t m", t=4), in_=ewg[:].rearrange("p (m t) -> p t m", t=4))
-        nc.vector.tensor_copy(out=esd[:].rearrange("p (t m) -> p m t", t=4), in_=esg[:].rearrange("p (m t) -> p m t", t=4))
+        nc.vector.tensor_copy(out=ewd[:].rearrange("p (t a m) -> p a t m", t=4, m=8), in_=ewg[:].rearrange("p (a m t) -> p a t m", t=4, m=8))
+        nc.vector.tensor_copy(out=esd[:].rearrange("p (t a m) -> p a t m", t=4, m=16), in_=esg[:].rearrange("p (a m t) -> p a t m", t=4, m=16))
+        for k in range(1, 4):
+            nc.sync.dma_start(out=esd[k:P:32, :].bitcast(I32), in_=esd[8 * k : P : 32, :].bitcast(I32))
+        trust_sb = keep.tile([P, G], F32, name="trust_sb", tag="short", align_bytes=64)
+        nc.sync.dma_start(out=trust_sb[:], in_=trust[0].partition_broadcast(P))
 
         win = [keep.tile([P, T], F32, name=f"win{u}", align_bytes=64) for u in range(2)]
         gat = [keep.tile([P, 2, CH], F32, name=f"gat{c}", align_bytes=64) for c in range(NCH)]
@@ -80,42 +83,50 @@ def tile_attend_coherence_pl_kernel(tc, ment, ents_words, ents_scales, comp, tru
         def gather(u, c):
             nc.vector.tensor_copy(out=gat[c][:, u, :], in_=win[u][:].indirect(offs2_sb[:, c * (CH // 16) : (c + 1) * (CH // 16)]))
 
-        cast(0)
-        cast(1)
-        cast(2)
+        for k in range(5):
+            cast(k)
         for c in range(NCH):
             gather(0, c)
-        for k in range(3, len(chunks)):
+        for k in range(5, len(chunks)):
             cast(k)
 
-        ment16 = keep.tile([P, G, 4], BF16, name="ment16", align_bytes=64)
-        nc.scalar.activation(out=ment16[:], in_=ment_raw[:].rearrange("p t g -> p g t"), func=ACT.Copy)
-
-        x16 = keep.tile([P, R, G * 4], BF16, name="x16", align_bytes=64)
-        xw = x16[:].bitcast(F32).rearrange("p (h q) (g u) -> p h g u q", q=4, u=2)
-        gc = CH // R
-        for c in range(NCH):
-            gather(1, c)
-            nc.scalar.copy(out=xw[:, :, gc * c : gc * (c + 1), :, :], in_=gat[c][:].rearrange("p u (g h q) -> p h g u q", h=2, q=4))
-
+        ment16 = [gat[2 + h][:, 1, 0:128].bitcast(BF16) for h in range(2)]
+        for h in range(2):
+            nc.scalar.activation(out=ment16[h].rearrange("p (g t) -> p g t", t=4), in_=ment_raw[:, :, 64 * h : 64 * (h + 1)].rearrange("p t g -> p g t"), func=ACT.Copy)
         mc = keep.tile([P, G], U32, name="mc", align_bytes=64)
         ms = keep.tile([P, G], U8, name="ms", align_bytes=64)
-        nc.vector.quantize_mx(out=mc[:].bitcast(FP8X4), scales=ms[:], in_=ment16[:].rearrange("p g t -> p (g t)"))
         a_ps = psum.tile([P, 4, G], F32, name="a_ps")
-        for t in range(4):
-            nc.tensor.matmul_mx(out=a_ps[:, t, :], lhsT=ewd[:, P * t : P * (t + 1)].bitcast(FP4X4), lhsT_scale=esd[:, P * t : P * (t + 1)],
-                                rhs=mc[:].bitcast(FP8X4), rhs_scale=ms[:], start=True, stop=True)
+
+        gc = CH // R
+
+        def weave(c, h, copy):
+            dst = x16[h][:].bitcast(F32).rearrange("p q (g u) -> p g u q", u=2)
+            src = gat[c][:].rearrange("p u (g h q) -> p h g u q", h=2, q=4)
+            copy(out=dst[:, gc * c : gc * (c + 1), :, :], in_=src[:, h, :, :, :])
+
+        for c in range(NCH):
+            if c == 2:
+                for h in range(2):
+                    nc.vector.quantize_mx(out=mc[:, 64 * h : 64 * (h + 1)].bitcast(FP8X4), scales=ms[:, 64 * h : 64 * (h + 1)], in_=ment16[h])
+                for rep in range(3):
+                    for t in range(4):
+                        nc.tensor.matmul_mx(out=a_ps[:, t, :], lhsT=ewd[:, P * t : P * (t + 1)].bitcast(FP4X4), lhsT_scale=esd[:, P * t : P * (t + 1)],
+                                            rhs=mc[:].bitcast(FP8X4), rhs_scale=ms[:], start=True, stop=True)
+            gather(1, c)
+            weave(c, 0, nc.scalar.copy if c < NCH - 1 else nc.vector.tensor_copy)
+            weave(c, 1, nc.scalar.copy)
 
         xc = keep.tile([P, R, G], U32, name="xc", align_bytes=64)
         xs = keep.tile([P, R, G], U8, name="xs", align_bytes=64)
-        for r in range(R):
-            nc.vector.quantize_mx(out=xc[:, r, :].bitcast(FP8X4), scales=xs[:, r, :], in_=x16[:, r, :])
+        for r0, r1 in ((0, 2), (2, 4), (4, 8)):
+            nc.vector.quantize_mx(out=xc[:, r0:r1, :].rearrange("p r g -> p (r g)").bitcast(FP8X4), scales=xs[:, r0:r1, :].rearrange("p r g -> p (r g)"),
+                                  in_=x16[r0 // 4][:, r0 % 4 : r0 % 4 + r1 - r0, :].rearrange("p r g -> p (r g)"))
 
         y = keep.tile([P, 4, G], F32, name="y")
         y16 = keep.tile([P, G, 4], BF16, name="y16", align_bytes=64)
         out_v = out_0.rearrange("(p t) g -> p t g", t=4)
-        for t in range(4):
-            b_ps = psum.tile([P, G], F32, name=f"b_ps{t}")
+        for n, t in enumerate((0, 1, 2, 3)):
+            b_ps = psum.tile([P, G], F32, name=f"b_ps{n % 3}")
             for r in range(R):
                 nc.tensor.matmul_mx(out=b_ps[:], lhsT=ewd[:, P * t : P * (t + 1)].bitcast(FP4X4), lhsT_scale=esd[:, P * t : P * (t + 1)],
                                     rhs=xc[:, r, :].bitcast(FP8X4), rhs_scale=xs[:, r, :], start=(r == 0), stop=(r == R - 1))
@@ -128,7 +139,7 @@ def tile_attend_coherence_pl_kernel(tc, ment, ents_words, ents_scales, comp, tru
             nc.vector.tensor_tensor(out=y[:, t, :], in0=tm[:], in1=a_ps[:, t, :], op=ALU.add)
             if t == 1:
                 nc.scalar.activation(out=y16[:, :, 0:2], in_=y[:, 0:2, :].rearrange("p t g -> p g t"), func=ACT.Copy)
-            if t == 2:
+            if n == 2:
                 nc.sync.dma_start(out=out_v[:, 0:3, :], in_=y[:, 0:3, :])
         nc.sync.dma_start(out=out_v[:, 3, :], in_=y[:, 3, :])
 

@@ -113,33 +113,37 @@ def tile_attend_coherence_pl_kernel(tc, ment, ents_words, ents_scales, comp, tru
                         nc.tensor.matmul_mx(out=a_ps[:, t, :], lhsT=ewd[:, P * t : P * (t + 1)].bitcast(FP4X4), lhsT_scale=esd[:, P * t : P * (t + 1)],
                                             rhs=mc[:].bitcast(FP8X4), rhs_scale=ms[:], start=True, stop=True)
             gather(1, c)
-            weave(c, 0, nc.scalar.copy if c < NCH - 1 else nc.vector.tensor_copy)
+            if c < NCH - 1:
+                weave(c, 0, nc.scalar.copy)
+            else:
+                dst = x16[0][:].bitcast(F32).rearrange("p (a q) (g u) -> p a g u q", a=2, u=2)
+                src = gat[c][:].rearrange("p u (g h a q) -> p h a g u q", h=2, a=2, q=2)
+                nc.vector.tensor_copy(out=dst[:, :, gc * c : gc * (c + 1), :, :], in_=src[:, 0, :, :, :, :])
             weave(c, 1, nc.scalar.copy)
 
         xc = keep.tile([P, R, G], U32, name="xc", align_bytes=64)
         xs = keep.tile([P, R, G], U8, name="xs", align_bytes=64)
-        for r0, r1 in ((0, 2), (2, 4), (4, 8)):
+        for r0, r1 in ((0, 1), (1, 2), (2, 4), (4, 8)):
             nc.vector.quantize_mx(out=xc[:, r0:r1, :].rearrange("p r g -> p (r g)").bitcast(FP8X4), scales=xs[:, r0:r1, :].rearrange("p r g -> p (r g)"),
                                   in_=x16[r0 // 4][:, r0 % 4 : r0 % 4 + r1 - r0, :].rearrange("p r g -> p (r g)"))
 
         y = keep.tile([P, 4, G], F32, name="y")
         y16 = keep.tile([P, G, 4], BF16, name="y16", align_bytes=64)
         out_v = out_0.rearrange("(p t) g -> p t g", t=4)
-        for n, t in enumerate((0, 1, 2, 3)):
-            b_ps = psum.tile([P, G], F32, name=f"b_ps{n % 3}")
+        tm = [keep.tile([P, 2, G], F32, name=f"tm{v}") for v in range(2)]
+        for t in range(4):
+            b_ps = psum.tile([P, G], F32, name=f"b_ps{t % 3}")
             for r in range(R):
                 nc.tensor.matmul_mx(out=b_ps[:], lhsT=ewd[:, P * t : P * (t + 1)].bitcast(FP4X4), lhsT_scale=esd[:, P * t : P * (t + 1)],
                                     rhs=xc[:, r, :].bitcast(FP8X4), rhs_scale=xs[:, r, :], start=(r == 0), stop=(r == R - 1))
             th = keep.tile([P, G], F32, name=f"th{t}")
-            tm = keep.tile([P, G], F32, name=f"tm{t}")
             nc.scalar.activation(out=th[:], in_=b_ps[:], func=ACT.Tanh, scale=1.0 / R)
-            nc.vector.tensor_tensor(out=tm[:], in0=th[:], in1=trust_sb[:], op=ALU.mult)
-            if t >= 2:
-                nc.vector.tensor_tensor(out=y16[:, :, t], in0=tm[:], in1=a_ps[:, t, :], op=ALU.add)
-            nc.vector.tensor_tensor(out=y[:, t, :], in0=tm[:], in1=a_ps[:, t, :], op=ALU.add)
-            if t == 1:
-                nc.scalar.activation(out=y16[:, :, 0:2], in_=y[:, 0:2, :].rearrange("p t g -> p g t"), func=ACT.Copy)
-            if n == 2:
+            nc.vector.tensor_tensor(out=tm[t // 2][:, t % 2, :], in0=th[:], in1=trust_sb[:], op=ALU.mult)
+            if t % 2 == 1:
+                nc.vector.tensor_tensor(out=y16[:, :, t - 1 : t + 1], in0=tm[t // 2][:].rearrange("p t g -> p g t"),
+                                        in1=a_ps[:, t - 1 : t + 1, :].rearrange("p t g -> p g t"), op=ALU.add)
+            nc.vector.tensor_tensor(out=y[:, t, :], in0=tm[t // 2][:, t % 2, :], in1=a_ps[:, t, :], op=ALU.add)
+            if t == 2:
                 nc.sync.dma_start(out=out_v[:, 0:3, :], in_=y[:, 0:3, :])
         nc.sync.dma_start(out=out_v[:, 3, :], in_=y[:, 3, :])
 

from contextlib import ExitStack

import concourse.mybir as mybir

D, T, I, J, G = 512, 2048, 512, 1024, 128
FLOPS = 2 * D * I * (J + G)

F32 = mybir.dt.float32
BF16 = mybir.dt.bfloat16
I32 = mybir.dt.int32
U32 = mybir.dt.uint32
U16 = mybir.dt.uint16
U8 = mybir.dt.uint8
FP8X4 = mybir.dt.float8_e4m3fn_x4
FP4X4 = mybir.dt.float4_e2m1fn_x4
ACT = mybir.ActivationFunctionType
ALU = mybir.AluOpType

P = 128
R = J // G
CH = 256
NCH = J // CH


def tile_attend_coherence_pl_kernel(tc, ment, ents_words, ents_scales, comp, trust, offs, offs2, out_0, out_1, out_2):
    nc = tc.nc
    with ExitStack() as ctx:
        keep = ctx.enter_context(tc.tile_pool(name="keep", bufs=1))
        shared = ctx.enter_context(tc.tile_pool(name="shared", bufs=1))
        psum = ctx.enter_context(tc.psum_pool(name="psum", bufs=1))

        offs_sb = keep.tile([P, I // 16], U16, name="offs_sb")
        offs2_sb = keep.tile([P, J // 16], U16, name="offs2_sb")
        ew = keep.tile([P, T], U16, name="ew", align_bytes=64)
        es = keep.tile([P, T], U8, name="es", align_bytes=64)
        warm_in = keep.tile([P, 1], F32, name="warm_in")
        warm_out = keep.tile([P, 1], F32, name="warm_out")

        nc.vector.memset(warm_in[:], 0.0)
        nc.scalar.activation(out=warm_out[:], in_=warm_in[:], func=ACT.Tanh)
        nc.vector.memset(es[:].bitcast(I32), 0)
        nc.scalar.dma_start(out=es[0:P:8, :].bitcast(I32), in_=ents_scales[0].bitcast(I32))

        comp_v = comp.rearrange("(p t) n -> p t n", t=4)
        chunks = [(0, 0, 512, 512), (0, 512, 512, 512), (0, 1024, 512, 256), (0, 1536, 512, 192), (1, 0, 512, 512), (1, 512, 512, 512), (1, 1024, 512, 192), (1, 1536, 256, 96), (1, 1792, 256, 96)]
        raw = [keep.tile([P, 2, w], F32, name=f"raw{k}") for k, (u, c0, w, s) in enumerate(chunks)]
        x16 = [shared.tile([P, 4, G * 4], BF16, name=f"x16_{h}", align_bytes=64, offset=4096 * h) for h in range(2)]
        ment_raw = shared.tile([P, 4, G], F32, name="ment_raw", align_bytes=64, offset=3072)

        for h in range(2):
            nc.sync.dma_start(out=ew[:].bitcast(I32)[:, 512 * h : 512 * (h + 1)], in_=ents_words[0].bitcast(I32)[:, 512 * h : 512 * (h + 1)])
        nc.sync.dma_start(offs_sb[:], offs)
        nc.sync.dma_start(offs2_sb[:], offs2)
        for k, (u, c0, w, s) in enumerate(chunks):
            nc.sync.dma_start(out=raw[k][:], in_=comp_v[:, 2 * u : 2 * u + 2, c0 : c0 + w])
        nc.sync.dma_start(out=ment_raw[:], in_=ment.rearrange("(p t) g -> p t g", t=4))

        ewg = keep.tile([P, I], U16, name="ewg", align_bytes=64)
        esg = keep.tile([P, I], U8, name="esg", tag="short", align_bytes=64)
        ewd = keep.tile([P, I], U16, name="ewd", align_bytes=64)
        esd = keep.tile([P, I], U8, name="esd", align_bytes=64)
        nc.vector.tensor_copy(out=ewg[:], in_=ew[:].indirect(offs_sb[:]))
        nc.vector.tensor_copy(out=esg[:], in_=es[:].indirect(offs_sb[:]))
        nc.vector.tensor_copy(out=ewd[:].rearrange("p (t a m) -> p a t m", t=4, m=8), in_=ewg[:].rearrange("p (a m t) -> p a t m", t=4, m=8))
        nc.vector.tensor_copy(out=esd[:].rearrange("p (t a m) -> p a t m", t=4, m=16), in_=esg[:].rearrange("p (a m t) -> p a t m", t=4, m=16))
        for k in range(1, 4):
            nc.sync.dma_start(out=esd[k:P:32, :].bitcast(I32), in_=esd[8 * k : P : 32, :].bitcast(I32))
        trust_sb = keep.tile([P, G], F32, name="trust_sb", tag="short", align_bytes=64)
        nc.sync.dma_start(out=trust_sb[:], in_=trust[0].partition_broadcast(P))

        win = [keep.tile([P, T], F32, name=f"win{u}", align_bytes=64) for u in range(2)]
        gat = [keep.tile([P, 2, CH], F32, name=f"gat{c}", align_bytes=64) for c in range(NCH)]

        def cast(k):
            u, c0, w, s = chunks[k]
            dst = win[u][:].bitcast(BF16).rearrange("p (n e) -> p n e", e=2)
            src = raw[k][:].rearrange("p e n -> p n e")
            if s > 0:
                nc.scalar.activation(out=dst[:, c0 : c0 + s, :], in_=src[:, 0:s, :], func=ACT.Copy)
            if s < w:
                nc.vector.tensor_copy(out=dst[:, c0 + s : c0 + w, :], in_=src[:, s:w, :])

        def gather(u, c):
            nc.vector.tensor_copy(out=gat[c][:, u, :], in_=win[u][:].indirect(offs2_sb[:, c * (CH // 16) : (c + 1) * (CH // 16)]))

        for k in range(5):
            cast(k)
        for c in range(NCH):
            gather(0, c)
        for k in range(5, len(chunks)):
            cast(k)

        ment16 = [gat[2 + h][:, 1, 0:128].bitcast(BF16) for h in range(2)]
        for h in range(2):
            nc.scalar.activation(out=ment16[h].rearrange("p (g t) -> p g t", t=4), in_=ment_raw[:, :, 64 * h : 64 * (h + 1)].rearrange("p t g -> p g t"), func=ACT.Copy)
        mc = keep.tile([P, G], U32, name="mc", align_bytes=64)
        ms = keep.tile([P, G], U8, name="ms", align_bytes=64)
        a_ps = psum.tile([P, 4, G], F32, name="a_ps")

        gc = CH // R

        def weave(c, h, copy):
            dst = x16[h][:].bitcast(F32).rearrange("p q (g u) -> p g u q", u=2)
            src = gat[c][:].rearrange("p u (g h q) -> p h g u q", h=2, q=4)
            copy(out=dst[:, gc * c : gc * (c + 1), :, :], in_=src[:, h, :, :, :])

        for c in range(NCH):
            if c == 2:
                for h in range(2):
                    nc.vector.quantize_mx(out=mc[:, 64 * h : 64 * (h + 1)].bitcast(FP8X4), scales=ms[:, 64 * h : 64 * (h + 1)], in_=ment16[h])
                for rep in range(3):
                    for t in range(4):
                        nc.tensor.matmul_mx(out=a_ps[:, t, :], lhsT=ewd[:, P * t : P * (t + 1)].bitcast(FP4X4), lhsT_scale=esd[:, P * t : P * (t + 1)],
                                            rhs=mc[:].bitcast(FP8X4), rhs_scale=ms[:], start=True, stop=True)
            gather(1, c)
            if c < NCH - 1:
                weave(c, 0, nc.scalar.copy)
            else:
                dst = x16[0][:].bitcast(F32).rearrange("p (a q) (g u) -> p a g u q", a=2, u=2)
                src = gat[c][:].rearrange("p u (g h a q) -> p h a g u q", h=2, a=2, q=2)
                nc.vector.tensor_copy(out=dst[:, :, gc * c : gc * (c + 1), :, :], in_=src[:, 0, :, :, :, :])
            weave(c, 1, nc.scalar.copy)

        xc = keep.tile([P, R, G], U32, name="xc", align_bytes=64)
        xs = keep.tile([P, R, G], U8, name="xs", align_bytes=64)
        for r0, r1 in ((0, 1), (1, 2), (2, 4), (4, 8)):
            nc.vector.quantize_mx(out=xc[:, r0:r1, :].rearrange("p r g -> p (r g)").bitcast(FP8X4), scales=xs[:, r0:r1, :].rearrange("p r g -> p (r g)"),
                                  in_=x16[r0 // 4][:, r0 % 4 : r0 % 4 + r1 - r0, :].rearrange("p r g -> p (r g)"))

        y = keep.tile([P, 4, G], F32, name="y")
        y16 = keep.tile([P, G, 4], BF16, name="y16", align_bytes=64)
        out_v = out_0.rearrange("(p t) g -> p t g", t=4)
        tm = [keep.tile([P, 2, G], F32, name=f"tm{v}") for v in range(2)]
        for t in range(4):
            b_ps = psum.tile([P, G], F32, name=f"b_ps{t % 3}")
            for r in range(R):
                nc.tensor.matmul_mx(out=b_ps[:], lhsT=ewd[:, P * t : P * (t + 1)].bitcast(FP4X4), lhsT_scale=esd[:, P * t : P * (t + 1)],
                                    rhs=xc[:, r, :].bitcast(FP8X4), rhs_scale=xs[:, r, :], start=(r == 0), stop=(r == R - 1))
            th = keep.tile([P, G], F32, name=f"th{t}")
            nc.scalar.activation(out=th[:], in_=b_ps[:], func=ACT.Tanh, scale=1.0 / R)
            nc.vector.tensor_tensor(out=tm[t // 2][:, t % 2, :], in0=th[:], in1=trust_sb[:], op=ALU.mult)
            if t % 2 == 1:
                nc.vector.tensor_tensor(out=y16[:, :, t - 1 : t + 1], in0=tm[t // 2][:].rearrange("p t g -> p g t"),
                                        in1=a_ps[:, t - 1 : t + 1, :].rearrange("p t g -> p g t"), op=ALU.add)
            nc.vector.tensor_tensor(out=y[:, t, :], in0=tm[t // 2][:, t % 2, :], in1=a_ps[:, t, :], op=ALU.add)
            if t == 2:
                nc.sync.dma_start(out=out_v[:, 0:3, :], in_=y[:, 0:3, :])
        nc.sync.dma_start(out=out_v[:, 3, :], in_=y[:, 3, :])

        yc = keep.tile([P, G], U32, name="yc", align_bytes=64)
        ys = keep.tile([P, G], U8, name="ys", align_bytes=64)
        nc.vector.quantize_mx(out=yc[:].bitcast(FP8X4), scales=ys[:], in_=y16[:].rearrange("p g t -> p (g t)"))
        nc.sync.dma_start(out=out_1[0].rearrange("p c r -> p (c r)").bitcast(I32), in_=yc[:].bitcast(I32))
        for q in range(4):
            eng = nc.scalar if q < 2 else nc.sync
            eng.dma_start(out=out_2[0, 4 * q : 4 * q + 4, :].bitcast(I32), in_=ys[32 * q : 32 * q + 4, :].bitcast(I32))
